import numpy as np
CORES = [24,48,72,96,120]
N = 5
def setup_inputs(rng):
    return {"x": rng.standard_normal((N, 128, 1024), dtype=np.float32)}
def reference(x):
    g = np.ascontiguousarray(x.transpose(1, 2, 0)).reshape(128, 1024 * N)
    return {"y": np.broadcast_to(g, (N,) + g.shape)}

@@ -1,0 +1,43 @@
+SCRATCH = {
+    "xs": ("sbuf", [128, 1024], "float32"),
+    "land0": ("sbuf", [128, 1024], "float32"),
+    "land1": ("sbuf", [128, 1024], "float32"),
+    "land2": ("sbuf", [128, 1024], "float32"),
+    "land3": ("sbuf", [128, 1024], "float32"),
+    "land4": ("sbuf", [128, 1024], "float32"),
+    "ys": ("sbuf", [128, 1024, 5], "float32"),
+}
+SEMAPHORES = ["loaded", "sent", "arrived", "woven", "stored"]
+
+
+def rank_program(g, core, T, topo):
+    rank = T.rank_of(core)
+    cores = T.cores
+    if rank is None:
+        if (core - 2) in cores:
+            owner = core - 2
+            r = T.rank_of(owner)
+            far = [c for c in cores if (topo.chip(c) & 1) != (topo.chip(owner) & 1)]
+            g.wait_ge(T.sem.arrived, 16)
+            for c in far:
+                rid, pid, _se = topo.addr(c)
+                g.remote_dma(T["land%d" % r][:], T.xs[:], T.sem.arrived, T.sem.sent, pid, rid, 0xFF)
+            g.wait_ge(T.sem.sent, 8 * len(far))
+        return
+    g.dma_start(T.xs[:], T.x[:]).then_inc(T.sem.loaded, 16)
+    g.wait_ge(T.sem.loaded, 16)
+    near = [c for c in cores if c != core and (topo.chip(c) & 1) == (topo.chip(core) & 1)]
+    rid, pid, _se = topo.addr(core + 2)
+    g.remote_dma(T.xs[:], T.xs[:], T.sem.arrived, T.sem.sent, pid, rid, 0xFFFF)
+    for c in near:
+        rid, pid, _se = topo.addr(c)
+        g.remote_dma(T["land%d" % rank][:], T.xs[:], T.sem.arrived, T.sem.sent, pid, rid, 0xFF)
+    g.wait_ge(T.sem.arrived, 32)
+    g.wait_ge(T.sem.sent, 16 + 8 * len(near))
+    for r in range(5):
+        src = T.xs if r == rank else T["land%d" % r]
+        for b in range(0, 1024, 64):
+            g.dma_start(T.ys[:, b:b + 64, r], src[:, b:b + 64], allow_slow_non_contiguous=True).then_inc(T.sem.woven, 16)
+    g.wait_ge(T.sem.woven, 80 * 16)
+    g.dma_start(T.y[:], T.ys[:]).then_inc(T.sem.stored, 16)
+    g.wait_ge(T.sem.stored, 16)

@@ -1,43 +1,127 @@
+from concourse.bass import DstId, RemoteDMATransfer
+
+NCORES = 128
+N = 5
 SCRATCH = {
-    "xs": ("sbuf", [128, 1024], "float32"),
-    "land0": ("sbuf", [128, 1024], "float32"),
-    "land1": ("sbuf", [128, 1024], "float32"),
-    "land2": ("sbuf", [128, 1024], "float32"),
-    "land3": ("sbuf", [128, 1024], "float32"),
-    "land4": ("sbuf", [128, 1024], "float32"),
-    "ys": ("sbuf", [128, 1024, 5], "float32"),
+    "xs": ("dram", [128, 128, 8], "float32"),
+    "land": ("dram", [N, 128, 8], "float32"),
+    "ystage": ("dram", [128, 128, 40], "float32"),
 }
-SEMAPHORES = ["loaded", "sent", "arrived", "woven", "stored"]
+SEMAPHORES = ["loaded", "sent", "rin", "near", "far", "woven", "arr0", "arr1", "arr2", "arr3", "stored"]
+
+
+def owns_mate_port(topo, c):
+    return topo.may_write(c, (c + 8) % NCORES)
+
+
+def weaver_order(topo):
+    quarters = [[], [], [], []]
+    for c in range(NCORES):
+        own = owns_mate_port(topo, c)
+        if topo.chip(c) & 1:
+            quarters[1 if own else 0].append(c)
+        else:
+            quarters[2 if own else 3].append(c)
+    return quarters[0] + quarters[1] + quarters[2] + quarters[3]
 
 
 def rank_program(g, core, T, topo):
     rank = T.rank_of(core)
-    cores = T.cores
-    if rank is None:
-        if (core - 2) in cores:
-            owner = core - 2
-            r = T.rank_of(owner)
-            far = [c for c in cores if (topo.chip(c) & 1) != (topo.chip(owner) & 1)]
-            g.wait_ge(T.sem.arrived, 16)
-            for c in far:
-                rid, pid, _se = topo.addr(c)
-                g.remote_dma(T["land%d" % r][:], T.xs[:], T.sem.arrived, T.sem.sent, pid, rid, 0xFF)
-            g.wait_ge(T.sem.sent, 8 * len(far))
-        return
-    g.dma_start(T.xs[:], T.x[:]).then_inc(T.sem.loaded, 16)
-    g.wait_ge(T.sem.loaded, 16)
-    near = [c for c in cores if c != core and (topo.chip(c) & 1) == (topo.chip(core) & 1)]
-    rid, pid, _se = topo.addr(core + 2)
-    g.remote_dma(T.xs[:], T.xs[:], T.sem.arrived, T.sem.sent, pid, rid, 0xFFFF)
-    for c in near:
-        rid, pid, _se = topo.addr(c)
-        g.remote_dma(T["land%d" % rank][:], T.xs[:], T.sem.arrived, T.sem.sent, pid, rid, 0xFF)
-    g.wait_ge(T.sem.arrived, 32)
-    g.wait_ge(T.sem.sent, 16 + 8 * len(near))
-    for r in range(5):
-        src = T.xs if r == rank else T["land%d" % r]
-        for b in range(0, 1024, 64):
-            g.dma_start(T.ys[:, b:b + 64, r], src[:, b:b + 64], allow_slow_non_contiguous=True).then_inc(T.sem.woven, 16)
-    g.wait_ge(T.sem.woven, 80 * 16)
-    g.dma_start(T.y[:], T.ys[:]).then_inc(T.sem.stored, 16)
-    g.wait_ge(T.sem.stored, 16)
+    order = weaver_order(topo)
+    row_of = {c: t for t, c in enumerate(order)}
+    t = row_of[core]
+    par = topo.chip(core) & 1
+    owner = owns_mate_port(topo, core)
+    near_ranks = [c for c in T.cores if (topo.chip(c) & 1) == par and c != core]
+    far_ranks = [c for c in T.cores if (topo.chip(c) & 1) != par]
+    sent = [0]
+
+    def transfer(dsts, mask, sem, src, dst_of):
+        ids = []
+        for c in dsts:
+            rid, pid, _se = topo.addr(c)
+            ids.append(DstId(rid=rid, pnc=pid))
+        sent[0] += bin(mask).count("1")
+        return RemoteDMATransfer(dst_ids=ids, dma_engine_mask=mask, remote_sem=sem,
+                                 srcs=[src], dsts=[dst_of() for _c in dsts])
+
+    def relayed_by(relay):
+        k = relay % 8
+        return [w for w in range(NCORES)
+                if (topo.chip(w) & 1) != (topo.chip(relay) & 1) and (w % 8) in (k - 2, k)]
+
+    if rank is not None:
+        g.dma_start(T.xs[:], T.x[:]).then_inc(T.sem.loaded, 16)
+        g.wait_ge(T.sem.loaded, 16)
+        chip0 = core - core % 8
+        on_chip = []
+        off_chip = []
+        for relay in range(chip0, chip0 + 8):
+            if owns_mate_port(topo, relay):
+                for w in relayed_by(relay):
+                    on_chip.append((relay, row_of[w], True))
+        for w in range(NCORES):
+            if (topo.chip(w) & 1) == par and w != core:
+                (on_chip if topo.chip(w) == topo.chip(core) else off_chip).append((w, row_of[w], False))
+
+        def row_transfer(item, engine):
+            dst, row, to_relay = item
+            if to_relay:
+                return transfer([dst], 1 << engine, T.sem.rin, T.xs[row], lambda: T.xs[row])
+            return transfer([dst], 1 << engine, T.sem.near, T.xs[row], lambda: T.land[rank])
+
+        g.remote_dma_fused([row_transfer(it, e) for e, it in enumerate(on_chip[:16])], local_sem=T.sem.sent)
+        on_chip = on_chip[16:]
+        while off_chip or on_chip:
+            call = [row_transfer(it, e) for e, it in enumerate(off_chip[:8])]
+            call += [row_transfer(it, 8 + e) for e, it in enumerate(on_chip[:8])]
+            off_chip = off_chip[8:]
+            on_chip = on_chip[8:]
+            g.remote_dma_fused(call, local_sem=T.sem.sent)
+
+    home = core - core % 8
+    if owner and T.rank_of(home) is not None:
+        r_home = T.rank_of(home)
+        rows = [(w, row_of[w]) for w in relayed_by(core)]
+        g.wait_ge(T.sem.rin, len(rows))
+        for k in range(0, len(rows), 8):
+            g.remote_dma_fused(
+                [transfer([w], 1 << e, T.sem.far, T.xs[row], lambda: T.land[r_home])
+                 for e, (w, row) in enumerate(rows[k:k + 8])], local_sem=T.sem.sent)
+
+    def weave(c):
+        r = T.rank_of(c)
+        src = T.xs[t] if c == core else T.land[r]
+        g.dma_start(T.ystage[t, :, r::N], src, allow_slow_non_contiguous=True).then_inc(T.sem.woven, 16)
+
+    if rank is not None:
+        weave(core)
+    g.wait_ge(T.sem.near, len(near_ranks))
+    for c in near_ranks:
+        weave(c)
+    g.wait_ge(T.sem.far, len(far_ranks))
+    for c in far_ranks:
+        weave(c)
+    g.wait_ge(T.sem.woven, 16 * N)
+
+    def deliver(row, dsts):
+        g.remote_dma_fused([transfer(dsts, 0xFF, T.sem["arr%d" % (row // 32)], T.ystage[row],
+                                     lambda: T.ystage[row])], local_sem=T.sem.sent)
+
+    if owner:
+        deliver(t, near_ranks + far_ranks)
+        nb = row_of[core - 2]
+        g.wait_ge(T.sem["arr%d" % (nb // 32)], 8)
+        deliver(nb, far_ranks)
+    else:
+        deliver(t, near_ranks + [core + 2])
+
+    if rank is not None:
+        g.sem_inc(T.sem["arr%d" % (t // 32)], 8)
+        early = [1, 0, 2] if par else [2, 3, 1]
+        late = 3 if par else 0
+        for queue, q in ((g.sync, early[0]), (g.scalar, early[1]), (g.sync, early[2]), (g.scalar, late)):
+            queue.wait_ge(T.sem["arr%d" % q], 8 * 32)
+            queue.dma_start(T.y[32 * q:32 * q + 32, :], T.ystage[32 * q:32 * q + 32]).then_inc(T.sem.stored, 16)
+        g.wait_ge(T.sem.stored, 64)
+    g.wait_ge(T.sem.sent, sent[0])

from concourse.bass import DstId, RemoteDMATransfer

NCORES = 128
N = 5
SCRATCH = {
    "xs": ("dram", [128, 128, 8], "float32"),
    "land": ("dram", [N, 128, 8], "float32"),
    "ystage": ("dram", [128, 128, 40], "float32"),
}
SEMAPHORES = ["loaded", "sent", "rin", "near", "far", "woven", "arr0", "arr1", "arr2", "arr3", "stored"]


def owns_mate_port(topo, c):
    return topo.may_write(c, (c + 8) % NCORES)


def weaver_order(topo):
    quarters = [[], [], [], []]
    for c in range(NCORES):
        own = owns_mate_port(topo, c)
        if topo.chip(c) & 1:
            quarters[1 if own else 0].append(c)
        else:
            quarters[2 if own else 3].append(c)
    return quarters[0] + quarters[1] + quarters[2] + quarters[3]


def rank_program(g, core, T, topo):
    rank = T.rank_of(core)
    order = weaver_order(topo)
    row_of = {c: t for t, c in enumerate(order)}
    t = row_of[core]
    par = topo.chip(core) & 1
    owner = owns_mate_port(topo, core)
    near_ranks = [c for c in T.cores if (topo.chip(c) & 1) == par and c != core]
    far_ranks = [c for c in T.cores if (topo.chip(c) & 1) != par]
    sent = [0]

    def transfer(dsts, mask, sem, src, dst_of):
        ids = []
        for c in dsts:
            rid, pid, _se = topo.addr(c)
            ids.append(DstId(rid=rid, pnc=pid))
        sent[0] += bin(mask).count("1")
        return RemoteDMATransfer(dst_ids=ids, dma_engine_mask=mask, remote_sem=sem,
                                 srcs=[src], dsts=[dst_of() for _c in dsts])

    def relayed_by(relay):
        k = relay % 8
        return [w for w in range(NCORES)
                if (topo.chip(w) & 1) != (topo.chip(relay) & 1) and (w % 8) in (k - 2, k)]

    if rank is not None:
        g.dma_start(T.xs[:], T.x[:]).then_inc(T.sem.loaded, 16)
        g.wait_ge(T.sem.loaded, 16)
        chip0 = core - core % 8
        on_chip = []
        off_chip = []
        for relay in range(chip0, chip0 + 8):
            if owns_mate_port(topo, relay):
                for w in relayed_by(relay):
                    on_chip.append((relay, row_of[w], True))
        for w in range(NCORES):
            if (topo.chip(w) & 1) == par and w != core:
                (on_chip if topo.chip(w) == topo.chip(core) else off_chip).append((w, row_of[w], False))

        def row_transfer(item, engine):
            dst, row, to_relay = item
            if to_relay:
                return transfer([dst], 1 << engine, T.sem.rin, T.xs[row], lambda: T.xs[row])
            return transfer([dst], 1 << engine, T.sem.near, T.xs[row], lambda: T.land[rank])

        g.remote_dma_fused([row_transfer(it, e) for e, it in enumerate(on_chip[:16])], local_sem=T.sem.sent)
        on_chip = on_chip[16:]
        while off_chip or on_chip:
            call = [row_transfer(it, e) for e, it in enumerate(off_chip[:8])]
            call += [row_transfer(it, 8 + e) for e, it in enumerate(on_chip[:8])]
            off_chip = off_chip[8:]
            on_chip = on_chip[8:]
            g.remote_dma_fused(call, local_sem=T.sem.sent)

    home = core - core % 8
    if owner and T.rank_of(home) is not None:
        r_home = T.rank_of(home)
        rows = [(w, row_of[w]) for w in relayed_by(core)]
        g.wait_ge(T.sem.rin, len(rows))
        for k in range(0, len(rows), 8):
            g.remote_dma_fused(
                [transfer([w], 1 << e, T.sem.far, T.xs[row], lambda: T.land[r_home])
                 for e, (w, row) in enumerate(rows[k:k + 8])], local_sem=T.sem.sent)

    def weave(c):
        r = T.rank_of(c)
        src = T.xs[t] if c == core else T.land[r]
        g.dma_start(T.ystage[t, :, r::N], src, allow_slow_non_contiguous=True).then_inc(T.sem.woven, 16)

    if rank is not None:
        weave(core)
    g.wait_ge(T.sem.near, len(near_ranks))
    for c in near_ranks:
        weave(c)
    g.wait_ge(T.sem.far, len(far_ranks))
    for c in far_ranks:
        weave(c)
    g.wait_ge(T.sem.woven, 16 * N)

    def deliver(row, dsts):
        g.remote_dma_fused([transfer(dsts, 0xFF, T.sem["arr%d" % (row // 32)], T.ystage[row],
                                     lambda: T.ystage[row])], local_sem=T.sem.sent)

    if owner:
        deliver(t, near_ranks + far_ranks)
        nb = row_of[core - 2]
        g.wait_ge(T.sem["arr%d" % (nb // 32)], 8)
        deliver(nb, far_ranks)
    else:
        deliver(t, near_ranks + [core + 2])

    if rank is not None:
        g.sem_inc(T.sem["arr%d" % (t // 32)], 8)
        early = [1, 0, 2] if par else [2, 3, 1]
        late = 3 if par else 0
        for queue, q in ((g.sync, early[0]), (g.scalar, early[1]), (g.sync, early[2]), (g.scalar, late)):
            queue.wait_ge(T.sem["arr%d" % q], 8 * 32)
            queue.dma_start(T.y[32 * q:32 * q + 32, :], T.ystage[32 * q:32 * q + 32]).then_inc(T.sem.stored, 16)
        g.wait_ge(T.sem.stored, 64)
    g.wait_ge(T.sem.sent, sent[0])
